import numpy as np
import ml_dtypes


def mxq(x, axis, fmt="e4m3"):
    dtype, down = {"e4m3": (ml_dtypes.float8_e4m3fn, 7), "e5m2": (ml_dtypes.float8_e5m2, 14)}[fmt]
    v = np.moveaxis(np.asarray(x, np.float32).astype(ml_dtypes.bfloat16).astype(np.float64), axis, -1)
    blocks = v.reshape(v.shape[:-1] + (-1, 32))
    amax = np.abs(blocks).max(-1, keepdims=True)
    byte = np.maximum(np.where(amax > 0, np.frexp(amax)[1] - 1 + 127, 0) - down, 1)
    scale = np.exp2(byte - 127.0)
    codes = (blocks / scale).astype(np.float32).astype(dtype).astype(np.float64)
    return np.moveaxis((codes * scale).reshape(v.shape), -1, axis)


WIDE = False


def mx_kscale(k):
    if not WIDE:
        return np.ones(k)
    levels = np.array([10, -10, 5, -5, 0])
    if k % 512:
        return np.exp2(np.random.permutation(np.resize(levels, k // 32))).repeat(32)
    a = np.empty((k // 512, 16))
    for p in range(k // 512):
        a[p, :8] = np.random.permutation(np.resize(levels, 8))
        for g in range(8):
            far = levels[np.abs(levels - a[p, g]) >= 10]
            a[p, g + 8] = far[np.random.randint(len(far))]
    return np.exp2(a.ravel()).repeat(32)


def f64(x):
    return np.asarray(x).astype(np.float64)


def striped(idx):
    return np.tile(idx.reshape(-1, 16).T, (8, 1)).astype(np.uint16)


def unstriped(offs):
    return offs[:16].T.reshape(-1).astype(np.int64)


def pack_weight(w):
    k, n = w.shape
    w = f64(np.asarray(w, np.float32).astype(ml_dtypes.bfloat16)).reshape(k // 32, 32, n)
    amax = np.abs(w).max(1)
    byte = np.clip(np.where(amax > 0, np.frexp(amax)[1] - 1 + 127 - 7, 1), 1, 254)
    scaled = (w * np.exp2(127.0 - byte)[:, None, :]).reshape(k, n).astype(np.float32)
    words = np.ascontiguousarray(scaled.reshape(k // 512, 128, 4, n).transpose(0, 1, 3, 2)).astype(ml_dtypes.float8_e4m3fn).view(np.uint8)
    return words, np.ascontiguousarray(byte.astype(np.uint8).reshape(k // 512, 16, n))


def unpack_weight(words, scales):
    g, p, n, _ = words.shape
    vals = np.ascontiguousarray(words).view(ml_dtypes.float8_e4m3fn).astype(np.float64) * np.repeat(np.exp2(scales.astype(np.float64) - 127.0), 8, axis=1)[..., None]
    return vals.transpose(0, 1, 3, 2).reshape(g * 512, n)


def silu(v):
    return v / (1.0 + np.exp(-np.maximum(v, -700.0)))


K, T, S, V, H, N, J, U = 1024, 2048, 512, 256, 512, 256, 512, 512


def setup_inputs():
    n = np.random.standard_normal
    s = mx_kscale(K)[:, None]
    u = mx_kscale(H)
    r = mx_kscale(J)[:, None]
    packed_w2 = pack_weight(n((H, N)) / np.sqrt(2 * H) / u[:, None])
    return {
        "xT": (n((K, T)) * s).astype(np.float32),
        "aT": (n((J, U)) * r).astype(np.float32),
        "w1": (n((K, H)) / np.sqrt(K) / s * u).astype(np.float32),
        "w3": (n((J, H)) / np.sqrt(J) / r).astype(np.float32),
        "w2_words": packed_w2[0],
        "w2_scales": packed_w2[1],
        "offs": striped(np.random.permutation(T)[:S]),
        "pos1": striped(np.random.permutation(S)[:V]),
        "pos2": striped(np.random.permutation(S)[:V]),
    }


def reference(xT, aT, w1, w3, w2_words, w2_scales, offs, pos1, pos2):
    xq = mxq(f64(xT)[:, unstriped(offs)], 0, "e4m3")
    h = silu(mxq(f64(w1), 0, "e4m3").T @ xq)
    f = mxq(f64(w3), 0, "e4m3").T @ mxq(f64(aT), 0, "e4m3")
    z = h[:, unstriped(pos1)] * f[:, :V] + h[:, unstriped(pos2)] * f[:, V:2 * V]
    return unpack_weight(w2_words, w2_scales).T @ mxq(z, 0, "e4m3")

@@ -1,0 +1,200 @@
+from contextlib import ExitStack
+
+import concourse.mybir as mybir
+
+K, T, S, V, H, N, J = 1024, 2048, 512, 256, 512, 256, 512
+FLOPS = 2 * (K * H * S + J * H * S + H * N * V)
+
+F32 = mybir.dt.float32
+BF16 = mybir.dt.bfloat16
+I32 = mybir.dt.int32
+U32 = mybir.dt.uint32
+U16 = mybir.dt.uint16
+U8 = mybir.dt.uint8
+FP8X4 = mybir.dt.float8_e4m3fn_x4
+MULT = mybir.AluOpType.mult
+ADD = mybir.AluOpType.add
+SILU = mybir.ActivationFunctionType.Silu
+
+P = 128
+PACK = 4
+HALF = 256
+
+
+def tile_picked_dime_none_e_kernel(
+    tc, xT, aT, w1, w3, w2_words, w2_scales, offs, pos1, pos2, out
+):
+    nc = tc.nc
+    with ExitStack() as ctx:
+        lists = ctx.enter_context(tc.tile_pool(name="lists", bufs=1))
+        sb = ctx.enter_context(tc.tile_pool(name="sb", bufs=1))
+        psum = ctx.enter_context(tc.psum_pool(name="psum", bufs=1))
+
+        def tile(name, shape, dtype):
+            return sb.tile(shape, dtype, name=name, align_bytes=64)
+
+        def quantize(name, grouped, width):
+            codes = tile(name + "_codes", [P, width], U32)
+            scales = tile(name + "_scales", [P, width], U8)
+            nc.vector.quantize_mx(out=codes[:].bitcast(FP8X4), scales=scales[:], in_=grouped)
+            return codes, scales
+
+        def product(acc, lhs, lhs_cols, rhs, start, stop):
+            nc.tensor.matmul_mx(
+                out=acc,
+                lhsT=lhs[0][:, lhs_cols].bitcast(FP8X4),
+                lhsT_scale=lhs[1][:, lhs_cols],
+                rhs=rhs[0][:].bitcast(FP8X4),
+                rhs_scale=rhs[1][:],
+                start=start,
+                stop=stop,
+            )
+
+        def block(t):
+            return slice(t * P, (t + 1) * P)
+
+        x_rows = xT.rearrange("(g p j) c -> g j p c", p=P, j=PACK)
+        w1_rows = w1.rearrange("(g p j) c -> g p j c", p=P, j=PACK)
+        w3_rows = w3.rearrange("(p j) c -> p j c", j=PACK)
+        a_rows = aT.rearrange("(p j) c -> p j c", j=PACK)
+
+        offs_sb = lists.tile([P, S // 16], U16, name="offs_sb")
+        pos_sb = [lists.tile([P, V // 16], U16, name="pos_sb%d" % d) for d in range(2)]
+        x_sb = [tile("x_sb%d" % i, [P, T], F32) for i in range(2 * PACK)]
+        w3_raw = tile("w3_raw", [P, PACK, H], F32)
+        a_raw = [tile("a_raw%d" % d, [P, PACK, V], F32) for d in range(2)]
+        w1_raw = [[tile("w1_raw%d%d" % (g, u), [P, PACK, HALF], F32) for u in range(2)] for g in range(2)]
+        w2_codes = tile("w2_codes", [P, N], U32)
+        w2_plane = tile("w2_plane", [P, N], U8)
+
+        def load_x(i):
+            nc.sync.dma_start(out=x_sb[i][:], in_=x_rows[i // PACK][i % PACK])
+
+        def load_w1(g, u):
+            nc.sync.dma_start(out=w1_raw[g][u][:], in_=w1_rows[g][:, :, u * HALF : (u + 1) * HALF])
+
+        def load_a(d):
+            nc.sync.dma_start(out=a_raw[d][:], in_=a_rows[:, :, d * V : (d + 1) * V])
+
+        zero_in = tile("zero_in", [P, 1], F32)
+        zero = tile("zero", [P, 1], F32)
+        nc.vector.memset(zero_in[:], 0.0)
+        nc.vector.memset(w2_plane[:].bitcast(I32), 0)
+        nc.scalar.activation(out=zero[:], in_=zero_in[:], func=SILU)
+
+        load_x(0)
+        nc.sync.dma_start(offs_sb[:], offs)
+        nc.sync.dma_start(out=w3_raw[:], in_=w3_rows)
+        load_x(1)
+        load_a(0)
+        load_x(2)
+        nc.sync.dma_start(pos_sb[0][:], pos1)
+        nc.sync.dma_start(pos_sb[1][:], pos2)
+        for i in range(3, 7):
+            load_x(i)
+        load_w1(0, 0)
+        load_x(7)
+        load_w1(0, 1)
+        load_w1(1, 0)
+        load_w1(1, 1)
+        load_a(1)
+        nc.sync.dma_start(
+            out=w2_codes[:].bitcast(I32), in_=w2_words[0].rearrange("p n r -> p (n r)").bitcast(I32)
+        )
+        for q in range(4):
+            nc.sync.dma_start(
+                out=w2_plane[32 * q : 32 * q + 4, :].bitcast(I32),
+                in_=w2_scales[0][4 * q : 4 * q + 4, :].bitcast(I32),
+            )
+
+        def deal(copy, grouped, raw, first, count):
+            copy(
+                out=grouped[:, :, first : first + count, :].rearrange("p t m j -> p m j t"),
+                in_=raw[:].rearrange("p j (m t) -> p m j t", t=PACK),
+            )
+
+        def weave(copy, grouped, raw):
+            copy(
+                out=grouped[:].rearrange("p (c i) j -> p c j i", i=4),
+                in_=raw[:].rearrange("p j (c i) -> p c j i", i=4),
+            )
+
+        xg = [tile("xg%d" % g, [P, S, PACK], BF16) for g in range(2)]
+
+        def gather_x(i):
+            nc.vector.tensor_copy(out=xg[i // PACK][:, :, i % PACK], in_=x_sb[i][:].indirect(offs_sb[:]))
+
+        f_sb = [tile("f_sb%d" % d, [P, PACK, V], F32) for d in range(2)]
+
+        def filters(d, w3q, aq):
+            for pair in range(2):
+                acc = psum.tile([P, 2, V], F32, name="f_ps%d%d" % (d, pair), tag="f_ps%d%d" % (d, pair))
+                for e in range(2):
+                    product(acc[:, e, :], w3q, block(2 * pair + e), aq, True, True)
+                nc.scalar.copy(out=f_sb[d][:, 2 * pair : 2 * pair + 2, :], in_=acc[:])
+
+        gather_x(0)
+        w3_grouped = tile("w3_grouped", [P, PACK, P, PACK], BF16)
+        deal(nc.scalar.copy, w3_grouped, w3_raw, 0, P)
+        gather_x(1)
+        a_grouped = [tile("a_grouped%d" % d, [P, V, PACK], BF16) for d in range(2)]
+        weave(nc.scalar.copy, a_grouped[0], a_raw[0])
+        gather_x(2)
+        w3q = quantize("w3", w3_grouped[:].rearrange("p t m j -> p (t m j)"), H)
+        gather_x(3)
+        aq0 = quantize("a0", a_grouped[0][:].rearrange("p c j -> p (c j)"), V)
+        filters(0, w3q, aq0)
+        gather_x(4)
+        xq0 = quantize("x0", xg[0][:].rearrange("p c j -> p (c j)"), S)
+        gather_x(5)
+        gather_x(6)
+        w1_grouped = [tile("w1_grouped%d" % g, [P, PACK, P, PACK], BF16) for g in range(2)]
+        deal(nc.scalar.copy, w1_grouped[0], w1_raw[0][0], 0, P // 2)
+        gather_x(7)
+        deal(nc.scalar.copy, w1_grouped[0], w1_raw[0][1], P // 2, P // 2)
+        xq1 = quantize("x1", xg[1][:].rearrange("p c j -> p (c j)"), S)
+        w1q0 = quantize("w10", w1_grouped[0][:].rearrange("p t m j -> p (t m j)"), H)
+        h_ps = [psum.tile([P, S], F32, name="h_ps%d" % t) for t in range(PACK)]
+        for t in range(PACK):
+            product(h_ps[t][:], w1q0, block(t), xq0, True, False)
+        deal(nc.scalar.copy, w1_grouped[1], w1_raw[1][0], 0, P // 2)
+        deal(nc.vector.tensor_copy, w1_grouped[1], w1_raw[1][1], P // 2, P // 2)
+        h_sb = [tile("h_sb%d" % t, [P, S], F32) for t in range(PACK)]
+        for t in range(PACK):
+            w1q1 = quantize("w11%d" % t, w1_grouped[1][:, t, :, :].rearrange("p m j -> p (m j)"), P)
+            product(h_ps[t][:], w1q1, slice(0, P), xq1, False, True)
+            nc.scalar.activation(out=h_sb[t][:], in_=h_ps[t][:], func=SILU, bias=zero[:])
+        weave(nc.vector.tensor_copy, a_grouped[1], a_raw[1])
+
+        terms = [tile("terms%d" % d, [P, PACK, V], F32) for d in range(2)]
+
+        def term(d, t):
+            nc.vector.tensor_tensor(terms[d][:, t, :], h_sb[t][:].indirect(pos_sb[d][:]), f_sb[d][:, t, :], MULT)
+
+        term(0, 0)
+        aq1 = quantize("a1", a_grouped[1][:].rearrange("p c j -> p (c j)"), V)
+        filters(1, w3q, aq1)
+        for t in range(1, PACK):
+            term(0, t)
+        for t in range(PACK):
+            term(1, t)
+
+        z = tile("z", [P, V, PACK], BF16)
+        nc.vector.tensor_tensor(
+            z[:].rearrange("p (c i) t -> p c t i", i=4),
+            terms[0][:].rearrange("p t (c i) -> p c t i", i=4),
+            terms[1][:].rearrange("p t (c i) -> p c t i", i=4),
+            ADD,
+        )
+        zq = quantize("z", z[:].rearrange("p c t -> p (c t)"), V)
+
+        for b in range(2):
+            acc = psum.tile([P, 2, V], F32, name="o_ps%d" % b, tag="f_ps0%d" % b)
+            product(acc[:, 0, :], (w2_codes, w2_plane), block(b), zq, True, True)
+            res = tile("res%d" % b, [P, V], F32)
+            if b == 0:
+                nc.vector.tensor_copy(out=res[:], in_=acc[:, 0, :])
+                nc.sync.dma_start(out=out[block(b), :], in_=res[:])
+            else:
+                nc.scalar.copy(out=res[:], in_=acc[:, 0, :])
+                nc.scalar.dma_start(out=out[block(b), :], in_=res[:])

@@ -18,7 +18,8 @@ SILU = mybir.ActivationFunctionType.Silu
 
 P = 128
 PACK = 4
-HALF = 256
+W1_SCALAR = 48
+W1_PIECES = ((0, 32), (32, 32), (64, 32), (96, 32))
 
 
 def tile_picked_dime_none_e_kernel(
@@ -39,13 +40,13 @@ def tile_picked_dime_none_e_kernel(
             nc.vector.quantize_mx(out=codes[:].bitcast(FP8X4), scales=scales[:], in_=grouped)
             return codes, scales
 
-        def product(acc, lhs, lhs_cols, rhs, start, stop):
+        def product(acc, lhs, lhs_cols, rhs, rhs_cols, start, stop):
             nc.tensor.matmul_mx(
                 out=acc,
                 lhsT=lhs[0][:, lhs_cols].bitcast(FP8X4),
                 lhsT_scale=lhs[1][:, lhs_cols],
-                rhs=rhs[0][:].bitcast(FP8X4),
-                rhs_scale=rhs[1][:],
+                rhs=rhs[0][:, rhs_cols].bitcast(FP8X4),
+                rhs_scale=rhs[1][:, rhs_cols],
                 start=start,
                 stop=stop,
             )
@@ -53,25 +54,33 @@ def tile_picked_dime_none_e_kernel(
         def block(t):
             return slice(t * P, (t + 1) * P)
 
-        x_rows = xT.rearrange("(g p j) c -> g j p c", p=P, j=PACK)
+        x_rows = xT.rearrange("(g p j) c -> g p j c", p=P, j=PACK)
         w1_rows = w1.rearrange("(g p j) c -> g p j c", p=P, j=PACK)
         w3_rows = w3.rearrange("(p j) c -> p j c", j=PACK)
         a_rows = aT.rearrange("(p j) c -> p j c", j=PACK)
 
         offs_sb = lists.tile([P, S // 16], U16, name="offs_sb")
         pos_sb = [lists.tile([P, V // 16], U16, name="pos_sb%d" % d) for d in range(2)]
-        x_sb = [tile("x_sb%d" % i, [P, T], F32) for i in range(2 * PACK)]
+        x_pair = [tile("x_pair%d" % i, [P, 2, T], F32) for i in range(3)]
+        x_last = [tile("x_last%d" % i, [P, T], F32) for i in range(2)]
+        x_sb = [x_pair[i // 2][:, i % 2, :] for i in range(6)] + [x_last[0][:], x_last[1][:]]
         w3_raw = tile("w3_raw", [P, PACK, H], F32)
-        a_raw = [tile("a_raw%d" % d, [P, PACK, V], F32) for d in range(2)]
-        w1_raw = [[tile("w1_raw%d%d" % (g, u), [P, PACK, HALF], F32) for u in range(2)] for g in range(2)]
+        a_raw = [tile("a_raw0", [P, PACK, V], F32)]
+        a_late = [tile("a_late%d" % u, [P, PACK, V // 2], F32) for u in range(2)]
+        w1_first = tile("w1_first", [P, PACK, H], F32)
+        w1_raw = [tile("w1_raw%d" % u, [P, PACK, PACK * count], F32) for u, (first, count) in enumerate(W1_PIECES)]
         w2_codes = tile("w2_codes", [P, N], U32)
         w2_plane = tile("w2_plane", [P, N], U8)
 
-        def load_x(i):
-            nc.sync.dma_start(out=x_sb[i][:], in_=x_rows[i // PACK][i % PACK])
+        def load_pair(i):
+            nc.sync.dma_start(out=x_pair[i][:], in_=x_rows[i // 2][:, 2 * (i % 2) : 2 * (i % 2) + 2, :])
 
-        def load_w1(g, u):
-            nc.sync.dma_start(out=w1_raw[g][u][:], in_=w1_rows[g][:, :, u * HALF : (u + 1) * HALF])
+        def load_last(i):
+            nc.sync.dma_start(out=x_last[i][:], in_=x_rows[1][:, 2 + i, :])
+
+        def load_w1(u):
+            first, count = W1_PIECES[u]
+            nc.sync.dma_start(out=w1_raw[u][:], in_=w1_rows[1][:, :, PACK * first : PACK * (first + count)])
 
         def load_a(d):
             nc.sync.dma_start(out=a_raw[d][:], in_=a_rows[:, :, d * V : (d + 1) * V])
@@ -82,22 +91,22 @@ def tile_picked_dime_none_e_kernel(
         nc.vector.memset(w2_plane[:].bitcast(I32), 0)
         nc.scalar.activation(out=zero[:], in_=zero_in[:], func=SILU)
 
-        load_x(0)
+        load_pair(0)
         nc.sync.dma_start(offs_sb[:], offs)
         nc.sync.dma_start(out=w3_raw[:], in_=w3_rows)
-        load_x(1)
+        load_pair(1)
         load_a(0)
-        load_x(2)
+        load_pair(2)
+        load_last(0)
+        nc.sync.dma_start(out=w1_first[:], in_=w1_rows[0])
+        load_last(1)
+        for u in range(len(W1_PIECES)):
+            load_w1(u)
+        for u in range(2):
+            first = V + u * V // 2
+            nc.sync.dma_start(out=a_late[u][:], in_=a_rows[:, :, first : first + V // 2])
         nc.sync.dma_start(pos_sb[0][:], pos1)
         nc.sync.dma_start(pos_sb[1][:], pos2)
-        for i in range(3, 7):
-            load_x(i)
-        load_w1(0, 0)
-        load_x(7)
-        load_w1(0, 1)
-        load_w1(1, 0)
-        load_w1(1, 1)
-        load_a(1)
         nc.sync.dma_start(
             out=w2_codes[:].bitcast(I32), in_=w2_words[0].rearrange("p n r -> p (n r)").bitcast(I32)
         )
@@ -110,7 +119,7 @@ def tile_picked_dime_none_e_kernel(
         def deal(copy, grouped, raw, first, count):
             copy(
                 out=grouped[:, :, first : first + count, :].rearrange("p t m j -> p m j t"),
-                in_=raw[:].rearrange("p j (m t) -> p m j t", t=PACK),
+                in_=raw.rearrange("p j (m t) -> p m j t", t=PACK),
             )
 
         def weave(copy, grouped, raw):
@@ -121,80 +130,123 @@ def tile_picked_dime_none_e_kernel(
 
         xg = [tile("xg%d" % g, [P, S, PACK], BF16) for g in range(2)]
 
-        def gather_x(i):
-            nc.vector.tensor_copy(out=xg[i // PACK][:, :, i % PACK], in_=x_sb[i][:].indirect(offs_sb[:]))
+        def gather_x(i, first=0, count=S):
+            nc.vector.tensor_copy(
+                out=xg[i // PACK][:, first : first + count, i % PACK],
+                in_=x_sb[i].indirect(offs_sb[:, first // 16 : (first + count) // 16]),
+            )
 
         f_sb = [tile("f_sb%d" % d, [P, PACK, V], F32) for d in range(2)]
 
         def filters(d, w3q, aq):
             for pair in range(2):
-                acc = psum.tile([P, 2, V], F32, name="f_ps%d%d" % (d, pair), tag="f_ps%d%d" % (d, pair))
+                acc = psum.tile([P, 2, V], F32, name="f_ps%d%d" % (d, pair), tag="f_ps%d" % pair)
                 for e in range(2):
-                    product(acc[:, e, :], w3q, block(2 * pair + e), aq, True, True)
+                    product(acc[:, e, :], w3q, block(2 * pair + e), aq, slice(0, V), True, True)
                 nc.scalar.copy(out=f_sb[d][:, 2 * pair : 2 * pair + 2, :], in_=acc[:])
 
         gather_x(0)
-        w3_grouped = tile("w3_grouped", [P, PACK, P, PACK], BF16)
-        deal(nc.scalar.copy, w3_grouped, w3_raw, 0, P)
         gather_x(1)
-        a_grouped = [tile("a_grouped%d" % d, [P, V, PACK], BF16) for d in range(2)]
-        weave(nc.scalar.copy, a_grouped[0], a_raw[0])
+        w3_grouped = tile("w3_grouped", [P, PACK, P, PACK], BF16)
+        deal(nc.scalar.copy, w3_grouped, w3_raw[:], 0, P)
+        a_grouped = [tile("a_grouped0", [P, V, PACK], BF16)]
+        late_grouped = [tile("late_grouped%d" % u, [P, V // 2, PACK], BF16) for u in range(2)]
         gather_x(2)
         w3q = quantize("w3", w3_grouped[:].rearrange("p t m j -> p (t m j)"), H)
         gather_x(3)
+        weave(nc.scalar.copy, a_grouped[0], a_raw[0])
         aq0 = quantize("a0", a_grouped[0][:].rearrange("p c j -> p (c j)"), V)
-        filters(0, w3q, aq0)
-        gather_x(4)
         xq0 = quantize("x0", xg[0][:].rearrange("p c j -> p (c j)"), S)
-        gather_x(5)
-        gather_x(6)
+        filters(0, w3q, aq0)
+        for i in (4, 5, 6):
+            gather_x(i)
         w1_grouped = [tile("w1_grouped%d" % g, [P, PACK, P, PACK], BF16) for g in range(2)]
-        deal(nc.scalar.copy, w1_grouped[0], w1_raw[0][0], 0, P // 2)
-        gather_x(7)
-        deal(nc.scalar.copy, w1_grouped[0], w1_raw[0][1], P // 2, P // 2)
-        xq1 = quantize("x1", xg[1][:].rearrange("p c j -> p (c j)"), S)
+        deal(nc.scalar.copy, w1_grouped[0], w1_first[:, :, 0 : PACK * W1_SCALAR], 0, W1_SCALAR)
+        deal(nc.vector.tensor_copy, w1_grouped[0], w1_first[:, :, PACK * W1_SCALAR : H], W1_SCALAR, P - W1_SCALAR)
         w1q0 = quantize("w10", w1_grouped[0][:].rearrange("p t m j -> p (t m j)"), H)
-        h_ps = [psum.tile([P, S], F32, name="h_ps%d" % t) for t in range(PACK)]
-        for t in range(PACK):
-            product(h_ps[t][:], w1q0, block(t), xq0, True, False)
-        deal(nc.scalar.copy, w1_grouped[1], w1_raw[1][0], 0, P // 2)
-        deal(nc.vector.tensor_copy, w1_grouped[1], w1_raw[1][1], P // 2, P // 2)
+        stretches = [(0, slice(0, S // 2)), (0, slice(S // 2, S))] + [(t, slice(0, S)) for t in range(1, PACK)]
+        h_ps = [
+            psum.tile([P, cols.stop - cols.start], F32, name="h_ps%d" % n, tag="h_ps%d" % n)
+            for n, (t, cols) in enumerate(stretches)
+        ]
+        for n, (t, cols) in enumerate(stretches):
+            product(h_ps[n][:], w1q0, block(t), xq0, cols, True, False)
+        gather_x(7, 0, S // 2)
+        gather_x(7, S // 2, S // 2)
+        x1_codes = tile("x1_codes", [P, S], U32)
+        x1_scales = tile("x1_scales", [P, S], U8)
+        for first in (0, S // 2):
+            cols = slice(first, first + S // 2)
+            nc.vector.quantize_mx(
+                out=x1_codes[:, cols].bitcast(FP8X4),
+                scales=x1_scales[:, cols],
+                in_=xg[1][:, cols, :].rearrange("p c j -> p (c j)"),
+            )
+        xq1 = (x1_codes, x1_scales)
+        for u, (first, count) in enumerate(W1_PIECES):
+            deal(nc.vector.tensor_copy if u == 3 else nc.scalar.copy, w1_grouped[1], w1_raw[u][:], first, count)
+        weave(nc.scalar.copy, late_grouped[0], a_late[0])
         h_sb = [tile("h_sb%d" % t, [P, S], F32) for t in range(PACK)]
         for t in range(PACK):
             w1q1 = quantize("w11%d" % t, w1_grouped[1][:, t, :, :].rearrange("p m j -> p (m j)"), P)
-            product(h_ps[t][:], w1q1, slice(0, P), xq1, False, True)
-            nc.scalar.activation(out=h_sb[t][:], in_=h_ps[t][:], func=SILU, bias=zero[:])
-        weave(nc.vector.tensor_copy, a_grouped[1], a_raw[1])
+            for n, (owner, cols) in enumerate(stretches):
+                if owner == t:
+                    product(h_ps[n][:], w1q1, slice(0, P), xq1, cols, False, True)
+                    nc.scalar.activation(out=h_sb[t][:, cols], in_=h_ps[n][:], func=SILU, bias=zero[:])
+        weave(nc.vector.tensor_copy, late_grouped[1], a_late[1])
+        a1_codes = tile("a1_codes", [P, V], U32)
+        a1_scales = tile("a1_scales", [P, V], U8)
+        for u in range(2):
+            cols = slice(u * V // 2, (u + 1) * V // 2)
+            nc.vector.quantize_mx(
+                out=a1_codes[:, cols].bitcast(FP8X4),
+                scales=a1_scales[:, cols],
+                in_=late_grouped[u][:].rearrange("p c j -> p (c j)"),
+            )
+        aq1 = (a1_codes, a1_scales)
 
         terms = [tile("terms%d" % d, [P, PACK, V], F32) for d in range(2)]
 
-        def term(d, t):
-            nc.vector.tensor_tensor(terms[d][:, t, :], h_sb[t][:].indirect(pos_sb[d][:]), f_sb[d][:, t, :], MULT)
+        def term(d, t, first=0, count=V):
+            cols = slice(first, first + count)
+            picked = h_sb[t][:].indirect(pos_sb[d][:, first // 16 : (first + count) // 16])
+            nc.vector.tensor_tensor(terms[d][:, t, cols], picked, f_sb[d][:, t, cols], MULT)
 
         term(0, 0)
-        aq1 = quantize("a1", a_grouped[1][:].rearrange("p c j -> p (c j)"), V)
         filters(1, w3q, aq1)
         for t in range(1, PACK):
             term(0, t)
-        for t in range(PACK):
+        for t in range(PACK - 1):
             term(1, t)
+        term(1, PACK - 1, 0, V // 2)
+        term(1, PACK - 1, V // 2, V // 2)
 
-        z = tile("z", [P, V, PACK], BF16)
-        nc.vector.tensor_tensor(
-            z[:].rearrange("p (c i) t -> p c t i", i=4),
-            terms[0][:].rearrange("p t (c i) -> p c t i", i=4),
-            terms[1][:].rearrange("p t (c i) -> p c t i", i=4),
-            ADD,
-        )
-        zq = quantize("z", z[:].rearrange("p c t -> p (c t)"), V)
+        z = [tile("z%d" % u, [P, V // 2, PACK], BF16) for u in range(2)]
+        halves = [slice(u * V // 2, (u + 1) * V // 2) for u in range(2)]
+        for u in range(2):
+            nc.vector.tensor_tensor(
+                z[u][:].rearrange("p (c i) t -> p c t i", i=4),
+                terms[0][:, :, halves[u]].rearrange("p t (c i) -> p c t i", i=4),
+                terms[1][:, :, halves[u]].rearrange("p t (c i) -> p c t i", i=4),
+                ADD,
+            )
+        zq = [quantize("z%d" % u, z[u][:].rearrange("p c t -> p (c t)"), V // 2) for u in range(2)]
+        w2q = (w2_codes, w2_plane)
+        whole = slice(0, V // 2)
 
+        acc = psum.tile([P, 2, V // 2], F32, name="o_ps", tag="h_ps0")
         for b in range(2):
-            acc = psum.tile([P, 2, V], F32, name="o_ps%d" % b, tag="f_ps0%d" % b)
-            product(acc[:, 0, :], (w2_codes, w2_plane), block(b), zq, True, True)
-            res = tile("res%d" % b, [P, V], F32)
+            product(acc[:, b, :], w2q, block(b), zq[0], whole, True, True)
+        res = tile("res", [P, 2, V // 2], F32)
+        nc.scalar.copy(out=res[:], in_=acc[:])
+        nc.sync.dma_start(out=out[:, halves[0]].rearrange("(b p) v -> p b v", p=P), in_=res[:])
+        for b in range(2):
+            end = psum.tile([P, V // 2], F32, name="end_ps%d" % b, tag="h_ps%d" % (b + 1))
+            product(end[:], w2q, block(b), zq[1], whole, True, True)
+            last = tile("last%d" % b, [P, V // 2], F32)
             if b == 0:
-                nc.vector.tensor_copy(out=res[:], in_=acc[:, 0, :])
-                nc.sync.dma_start(out=out[block(b), :], in_=res[:])
+                nc.vector.tensor_copy(out=last[:], in_=end[:])
+                nc.sync.dma_start(out=out[block(b), halves[1]], in_=last[:])
             else:
-                nc.scalar.copy(out=res[:], in_=acc[:, 0, :])
-                nc.scalar.dma_start(out=out[block(b), :], in_=res[:])
+                nc.scalar.copy(out=last[:], in_=end[:])
+                nc.scalar.dma_start(out=out[block(b), halves[1]], in_=last[:])

from contextlib import ExitStack

import concourse.mybir as mybir

K, T, S, V, H, N, J = 1024, 2048, 512, 256, 512, 256, 512
FLOPS = 2 * (K * H * S + J * H * S + H * N * V)

F32 = mybir.dt.float32
BF16 = mybir.dt.bfloat16
I32 = mybir.dt.int32
U32 = mybir.dt.uint32
U16 = mybir.dt.uint16
U8 = mybir.dt.uint8
FP8X4 = mybir.dt.float8_e4m3fn_x4
MULT = mybir.AluOpType.mult
ADD = mybir.AluOpType.add
SILU = mybir.ActivationFunctionType.Silu

P = 128
PACK = 4
W1_SCALAR = 48
W1_PIECES = ((0, 32), (32, 32), (64, 32), (96, 32))


def tile_picked_dime_none_e_kernel(
    tc, xT, aT, w1, w3, w2_words, w2_scales, offs, pos1, pos2, out
):
    nc = tc.nc
    with ExitStack() as ctx:
        lists = ctx.enter_context(tc.tile_pool(name="lists", bufs=1))
        sb = ctx.enter_context(tc.tile_pool(name="sb", bufs=1))
        psum = ctx.enter_context(tc.psum_pool(name="psum", bufs=1))

        def tile(name, shape, dtype):
            return sb.tile(shape, dtype, name=name, align_bytes=64)

        def quantize(name, grouped, width):
            codes = tile(name + "_codes", [P, width], U32)
            scales = tile(name + "_scales", [P, width], U8)
            nc.vector.quantize_mx(out=codes[:].bitcast(FP8X4), scales=scales[:], in_=grouped)
            return codes, scales

        def product(acc, lhs, lhs_cols, rhs, rhs_cols, start, stop):
            nc.tensor.matmul_mx(
                out=acc,
                lhsT=lhs[0][:, lhs_cols].bitcast(FP8X4),
                lhsT_scale=lhs[1][:, lhs_cols],
                rhs=rhs[0][:, rhs_cols].bitcast(FP8X4),
                rhs_scale=rhs[1][:, rhs_cols],
                start=start,
                stop=stop,
            )

        def block(t):
            return slice(t * P, (t + 1) * P)

        x_rows = xT.rearrange("(g p j) c -> g p j c", p=P, j=PACK)
        w1_rows = w1.rearrange("(g p j) c -> g p j c", p=P, j=PACK)
        w3_rows = w3.rearrange("(p j) c -> p j c", j=PACK)
        a_rows = aT.rearrange("(p j) c -> p j c", j=PACK)

        offs_sb = lists.tile([P, S // 16], U16, name="offs_sb")
        pos_sb = [lists.tile([P, V // 16], U16, name="pos_sb%d" % d) for d in range(2)]
        x_pair = [tile("x_pair%d" % i, [P, 2, T], F32) for i in range(3)]
        x_last = [tile("x_last%d" % i, [P, T], F32) for i in range(2)]
        x_sb = [x_pair[i // 2][:, i % 2, :] for i in range(6)] + [x_last[0][:], x_last[1][:]]
        w3_raw = tile("w3_raw", [P, PACK, H], F32)
        a_raw = [tile("a_raw0", [P, PACK, V], F32)]
        a_late = [tile("a_late%d" % u, [P, PACK, V // 2], F32) for u in range(2)]
        w1_first = tile("w1_first", [P, PACK, H], F32)
        w1_raw = [tile("w1_raw%d" % u, [P, PACK, PACK * count], F32) for u, (first, count) in enumerate(W1_PIECES)]
        w2_codes = tile("w2_codes", [P, N], U32)
        w2_plane = tile("w2_plane", [P, N], U8)

        def load_pair(i):
            nc.sync.dma_start(out=x_pair[i][:], in_=x_rows[i // 2][:, 2 * (i % 2) : 2 * (i % 2) + 2, :])

        def load_last(i):
            nc.sync.dma_start(out=x_last[i][:], in_=x_rows[1][:, 2 + i, :])

        def load_w1(u):
            first, count = W1_PIECES[u]
            nc.sync.dma_start(out=w1_raw[u][:], in_=w1_rows[1][:, :, PACK * first : PACK * (first + count)])

        def load_a(d):
            nc.sync.dma_start(out=a_raw[d][:], in_=a_rows[:, :, d * V : (d + 1) * V])

        zero_in = tile("zero_in", [P, 1], F32)
        zero = tile("zero", [P, 1], F32)
        nc.vector.memset(zero_in[:], 0.0)
        nc.vector.memset(w2_plane[:].bitcast(I32), 0)
        nc.scalar.activation(out=zero[:], in_=zero_in[:], func=SILU)

        load_pair(0)
        nc.sync.dma_start(offs_sb[:], offs)
        nc.sync.dma_start(out=w3_raw[:], in_=w3_rows)
        load_pair(1)
        load_a(0)
        load_pair(2)
        load_last(0)
        nc.sync.dma_start(out=w1_first[:], in_=w1_rows[0])
        load_last(1)
        for u in range(len(W1_PIECES)):
            load_w1(u)
        for u in range(2):
            first = V + u * V // 2
            nc.sync.dma_start(out=a_late[u][:], in_=a_rows[:, :, first : first + V // 2])
        nc.sync.dma_start(pos_sb[0][:], pos1)
        nc.sync.dma_start(pos_sb[1][:], pos2)
        nc.sync.dma_start(
            out=w2_codes[:].bitcast(I32), in_=w2_words[0].rearrange("p n r -> p (n r)").bitcast(I32)
        )
        for q in range(4):
            nc.sync.dma_start(
                out=w2_plane[32 * q : 32 * q + 4, :].bitcast(I32),
                in_=w2_scales[0][4 * q : 4 * q + 4, :].bitcast(I32),
            )

        def deal(copy, grouped, raw, first, count):
            copy(
                out=grouped[:, :, first : first + count, :].rearrange("p t m j -> p m j t"),
                in_=raw.rearrange("p j (m t) -> p m j t", t=PACK),
            )

        def weave(copy, grouped, raw):
            copy(
                out=grouped[:].rearrange("p (c i) j -> p c j i", i=4),
                in_=raw[:].rearrange("p j (c i) -> p c j i", i=4),
            )

        xg = [tile("xg%d" % g, [P, S, PACK], BF16) for g in range(2)]

        def gather_x(i, first=0, count=S):
            nc.vector.tensor_copy(
                out=xg[i // PACK][:, first : first + count, i % PACK],
                in_=x_sb[i].indirect(offs_sb[:, first // 16 : (first + count) // 16]),
            )

        f_sb = [tile("f_sb%d" % d, [P, PACK, V], F32) for d in range(2)]

        def filters(d, w3q, aq):
            for pair in range(2):
                acc = psum.tile([P, 2, V], F32, name="f_ps%d%d" % (d, pair), tag="f_ps%d" % pair)
                for e in range(2):
                    product(acc[:, e, :], w3q, block(2 * pair + e), aq, slice(0, V), True, True)
                nc.scalar.copy(out=f_sb[d][:, 2 * pair : 2 * pair + 2, :], in_=acc[:])

        gather_x(0)
        gather_x(1)
        w3_grouped = tile("w3_grouped", [P, PACK, P, PACK], BF16)
        deal(nc.scalar.copy, w3_grouped, w3_raw[:], 0, P)
        a_grouped = [tile("a_grouped0", [P, V, PACK], BF16)]
        late_grouped = [tile("late_grouped%d" % u, [P, V // 2, PACK], BF16) for u in range(2)]
        gather_x(2)
        w3q = quantize("w3", w3_grouped[:].rearrange("p t m j -> p (t m j)"), H)
        gather_x(3)
        weave(nc.scalar.copy, a_grouped[0], a_raw[0])
        aq0 = quantize("a0", a_grouped[0][:].rearrange("p c j -> p (c j)"), V)
        xq0 = quantize("x0", xg[0][:].rearrange("p c j -> p (c j)"), S)
        filters(0, w3q, aq0)
        for i in (4, 5, 6):
            gather_x(i)
        w1_grouped = [tile("w1_grouped%d" % g, [P, PACK, P, PACK], BF16) for g in range(2)]
        deal(nc.scalar.copy, w1_grouped[0], w1_first[:, :, 0 : PACK * W1_SCALAR], 0, W1_SCALAR)
        deal(nc.vector.tensor_copy, w1_grouped[0], w1_first[:, :, PACK * W1_SCALAR : H], W1_SCALAR, P - W1_SCALAR)
        w1q0 = quantize("w10", w1_grouped[0][:].rearrange("p t m j -> p (t m j)"), H)
        stretches = [(0, slice(0, S // 2)), (0, slice(S // 2, S))] + [(t, slice(0, S)) for t in range(1, PACK)]
        h_ps = [
            psum.tile([P, cols.stop - cols.start], F32, name="h_ps%d" % n, tag="h_ps%d" % n)
            for n, (t, cols) in enumerate(stretches)
        ]
        for n, (t, cols) in enumerate(stretches):
            product(h_ps[n][:], w1q0, block(t), xq0, cols, True, False)
        gather_x(7, 0, S // 2)
        gather_x(7, S // 2, S // 2)
        x1_codes = tile("x1_codes", [P, S], U32)
        x1_scales = tile("x1_scales", [P, S], U8)
        for first in (0, S // 2):
            cols = slice(first, first + S // 2)
            nc.vector.quantize_mx(
                out=x1_codes[:, cols].bitcast(FP8X4),
                scales=x1_scales[:, cols],
                in_=xg[1][:, cols, :].rearrange("p c j -> p (c j)"),
            )
        xq1 = (x1_codes, x1_scales)
        for u, (first, count) in enumerate(W1_PIECES):
            deal(nc.vector.tensor_copy if u == 3 else nc.scalar.copy, w1_grouped[1], w1_raw[u][:], first, count)
        weave(nc.scalar.copy, late_grouped[0], a_late[0])
        h_sb = [tile("h_sb%d" % t, [P, S], F32) for t in range(PACK)]
        for t in range(PACK):
            w1q1 = quantize("w11%d" % t, w1_grouped[1][:, t, :, :].rearrange("p m j -> p (m j)"), P)
            for n, (owner, cols) in enumerate(stretches):
                if owner == t:
                    product(h_ps[n][:], w1q1, slice(0, P), xq1, cols, False, True)
                    nc.scalar.activation(out=h_sb[t][:, cols], in_=h_ps[n][:], func=SILU, bias=zero[:])
        weave(nc.vector.tensor_copy, late_grouped[1], a_late[1])
        a1_codes = tile("a1_codes", [P, V], U32)
        a1_scales = tile("a1_scales", [P, V], U8)
        for u in range(2):
            cols = slice(u * V // 2, (u + 1) * V // 2)
            nc.vector.quantize_mx(
                out=a1_codes[:, cols].bitcast(FP8X4),
                scales=a1_scales[:, cols],
                in_=late_grouped[u][:].rearrange("p c j -> p (c j)"),
            )
        aq1 = (a1_codes, a1_scales)

        terms = [tile("terms%d" % d, [P, PACK, V], F32) for d in range(2)]

        def term(d, t, first=0, count=V):
            cols = slice(first, first + count)
            picked = h_sb[t][:].indirect(pos_sb[d][:, first // 16 : (first + count) // 16])
            nc.vector.tensor_tensor(terms[d][:, t, cols], picked, f_sb[d][:, t, cols], MULT)

        term(0, 0)
        filters(1, w3q, aq1)
        for t in range(1, PACK):
            term(0, t)
        for t in range(PACK - 1):
            term(1, t)
        term(1, PACK - 1, 0, V // 2)
        term(1, PACK - 1, V // 2, V // 2)

        z = [tile("z%d" % u, [P, V // 2, PACK], BF16) for u in range(2)]
        halves = [slice(u * V // 2, (u + 1) * V // 2) for u in range(2)]
        for u in range(2):
            nc.vector.tensor_tensor(
                z[u][:].rearrange("p (c i) t -> p c t i", i=4),
                terms[0][:, :, halves[u]].rearrange("p t (c i) -> p c t i", i=4),
                terms[1][:, :, halves[u]].rearrange("p t (c i) -> p c t i", i=4),
                ADD,
            )
        zq = [quantize("z%d" % u, z[u][:].rearrange("p c t -> p (c t)"), V // 2) for u in range(2)]
        w2q = (w2_codes, w2_plane)
        whole = slice(0, V // 2)

        acc = psum.tile([P, 2, V // 2], F32, name="o_ps", tag="h_ps0")
        for b in range(2):
            product(acc[:, b, :], w2q, block(b), zq[0], whole, True, True)
        res = tile("res", [P, 2, V // 2], F32)
        nc.scalar.copy(out=res[:], in_=acc[:])
        nc.sync.dma_start(out=out[:, halves[0]].rearrange("(b p) v -> p b v", p=P), in_=res[:])
        for b in range(2):
            end = psum.tile([P, V // 2], F32, name="end_ps%d" % b, tag="h_ps%d" % (b + 1))
            product(end[:], w2q, block(b), zq[1], whole, True, True)
            last = tile("last%d" % b, [P, V // 2], F32)
            if b == 0:
                nc.vector.tensor_copy(out=last[:], in_=end[:])
                nc.sync.dma_start(out=out[block(b), halves[1]], in_=last[:])
            else:
                nc.scalar.copy(out=last[:], in_=end[:])
                nc.scalar.dma_start(out=out[block(b), halves[1]], in_=last[:])
